import numpy as np, ml_dtypes
CORES = [16,32,48,64,80]
N = 5
import mx_ref
NC, G = 128, 2
C = np.float32(0.023)
BF = ml_dtypes.bfloat16
def cut(t, i, w=512):
    return t[:, w * i:w * i + w]
def tile(rs):
    return np.stack(rs, axis=2).reshape(128, -1).astype(BF)
def act(Z):
    return [np.maximum(s * z, 0) * C for z in Z for s in (1, -1)]
def setup_inputs(rng):
    def f(*shape):
        return mx_ref.flush((rng.standard_normal(shape, dtype=np.float32) * np.exp2(rng.integers(-2, 3, shape[:-1] + (1,)))).astype(BF))
    return {"x": f(N, 128, 4 * NC), "res": f(N, 128, 4 * NC), "w1": f(N, 128, 512), "w2": f(N, 128, 2 * 512)}
def setup_inputs_blocks(rng):
    d = setup_inputs(rng)
    for k in ("x", "w1", "w2", "res"): d[k] = mx_ref.spread(d[k], rng, 4)
    return d
def setup_inputs_wide(rng):
    d = setup_inputs(rng)
    for k in ("x", "w1", "w2", "res"): d[k] = mx_ref.flush((d[k].astype(np.float32) * np.exp2(rng.integers(-6, 7, (N, 1, 1))).astype(np.float32)).astype(BF))
    return d
def reference(x, res, w1, w2):
    W = [mx_ref.quantize(w1[j]) for j in range(N)]; H = []
    for r in range(N):
        X = mx_ref.quantize(x[r]); e = res[r].astype(np.float32)
        R = act([mx_ref.matmul(W[(r + i) % N], X) for i in range(G)])
        H.append(mx_ref.quantize(tile([R[b] + e[:, b::4] for b in range(4)])))
    y = np.zeros((N, 128, NC), np.float32)
    for r in range(N):
        y[r] = mx_ref.matmul(mx_ref.quantize(cut(w2[r], 0)), H[r]) + mx_ref.matmul(mx_ref.quantize(cut(w2[r], 1)), H[(r + 1) % N])
    return {"y": y}

import numpy as np
from concourse.mybir import dt, AluOpType, ActivationFunctionType

NC = 128
C = float(np.float32(0.023))

SCRATCH = {
    "w1b": ("sbuf", [128, 4 * NC], "bfloat16"),
    "xb": ("sbuf", [128, 4 * NC], "bfloat16"),
    "resb": ("sbuf", [128, 4 * NC], "bfloat16"),
    "w2b": ("sbuf", [128, 8 * NC], "bfloat16"),
    "qw1": ("sbuf", [128, NC], "float8_e4m3fn_x4"), "sw1": ("sbuf", [128, NC], "uint8"),
    "qx": ("sbuf", [128, NC], "float8_e4m3fn_x4"), "sx": ("sbuf", [128, NC], "uint8"),
    "qw2": ("sbuf", [128, 2 * NC], "float8_e4m3fn_x4"), "sw2": ("sbuf", [128, 2 * NC], "uint8"),
    "qh": ("sbuf", [128, NC], "float8_e4m3fn_x4"), "sh": ("sbuf", [128, NC], "uint8"),
    "nw1": ("sbuf", [128, NC], "float8_e4m3fn_x4"), "nsw1": ("sbuf", [128, NC], "uint8"),
    "nqh": ("sbuf", [128, NC], "float8_e4m3fn_x4"), "nsh": ("sbuf", [128, NC], "uint8"),
    "a": ("sbuf", [128, 4 * NC], "float32"),
    "h": ("sbuf", [128, 4 * NC], "bfloat16"),
    "ysb": ("sbuf", [128, NC], "float32"),
    "ps": ("psum", [128, 3 * 512], "float32"),
}
SEMAPHORES = ["ld_w1", "ld_x", "ld_res", "ld_w2", "q1", "qx", "qw2", "qh", "z0", "z1", "a0", "a1", "a2", "a3", "hd",
              "w1in", "hin", "sent", "yd", "yc", "st"]


def _engines(mask):
    return bin(mask).count("1")


def rank_program(g, core, T, topo):
    rank = T.rank_of(core)
    if rank is None:
        return
    n = len(T.cores)
    dst = T.cores[(rank - 1) % n]
    src = T.cores[(rank + 1) % n]
    rid, pid, _ = topo.addr(dst)
    mask = topo.mask(core, dst)
    n_out = _engines(mask)
    n_in = _engines(topo.mask(src, core))
    S, u8 = T.sem, dt.uint8
    v, s, t, q = g.vector, g.scalar, g.tensor, g.sync
    relu = ActivationFunctionType.Relu

    def blk(b):
        return T.a[:, b * NC:(b + 1) * NC]

    def col(buf, b):
        return buf[:, b:4 * NC:4]

    z0, z1, yp = T.ps[:, 0:NC], T.ps[:, 512:512 + NC], T.ps[:, 1024:1024 + NC]

    q.dma_start(T.w1b[:], T.w1[:]).then_inc(S.ld_w1, 16)
    q.dma_start(T.xb[:], T.x[:]).then_inc(S.ld_x, 16)
    q.dma_start(T.resb[:], T.res[:]).then_inc(S.ld_res, 16)
    q.dma_start(T.w2b[:], T.w2[:]).then_inc(S.ld_w2, 16)
    q.wait_ge(S.yc, 1)
    q.dma_start(T.y[:], T.ysb[:]).then_inc(S.st, 16)
    q.wait_ge(S.st, 16)

    g.wait_ge(S.q1, 1)
    g.remote_dma(T.nw1[:].bitcast(u8), T.qw1[:].bitcast(u8), S.w1in, S.sent, pid, rid, mask)
    g.remote_dma(T.nsw1[:], T.sw1[:], S.w1in, S.sent, pid, rid, mask)
    g.wait_ge(S.qh, 1)
    g.remote_dma(T.nqh[:].bitcast(u8), T.qh[:].bitcast(u8), S.hin, S.sent, pid, rid, mask)
    g.remote_dma(T.nsh[:], T.sh[:], S.hin, S.sent, pid, rid, mask)
    g.wait_ge(S.sent, 4 * n_out)

    t.wait_ge(S.q1, 1)
    t.wait_ge(S.qx, 1)
    t.matmul_mx(z0, T.qw1[:], T.sw1[:], T.qx[:], T.sx[:], True, True).then_inc(S.z0, 1)
    t.wait_ge(S.w1in, 2 * n_in)
    t.matmul_mx(z1, T.nw1[:], T.nsw1[:], T.qx[:], T.sx[:], True, True).then_inc(S.z1, 1)
    t.wait_ge(S.qh, 1)
    t.wait_ge(S.qw2, 1)
    t.matmul_mx(yp, T.qw2[:, 0:NC], T.sw2[:, 0:NC], T.qh[:], T.sh[:], True, False)
    t.wait_ge(S.hin, 2 * n_in)
    t.matmul_mx(yp, T.qw2[:, NC:2 * NC], T.sw2[:, NC:2 * NC], T.nqh[:], T.nsh[:], False, True).then_inc(S.yd, 1)

    s.wait_ge(S.z0, 1)
    s.activation(blk(0), z0, relu, scale=C).then_inc(S.a0, 1)
    s.activation(blk(1), z0, relu, scale=-C).then_inc(S.a1, 1)
    s.wait_ge(S.z1, 1)
    s.activation(blk(2), z1, relu, scale=C).then_inc(S.a2, 1)
    s.activation(blk(3), z1, relu, scale=-C).then_inc(S.a3, 1)

    v.wait_ge(S.ld_w1, 16)
    v.quantize_mx(T.qw1[:], T.sw1[:], T.w1b[:]).then_inc(S.q1, 1)
    v.wait_ge(S.ld_x, 16)
    v.quantize_mx(T.qx[:], T.sx[:], T.xb[:]).then_inc(S.qx, 1)
    v.wait_ge(S.ld_res, 16)
    for b, sem in enumerate((S.a0, S.a1, S.a2, S.a3)):
        v.wait_ge(sem, 1)
        v.tensor_tensor(col(T.h, b), blk(b), col(T.resb, b), AluOpType.add).then_inc(S.hd, 1)
    v.wait_ge(S.hd, 4)
    v.quantize_mx(T.qh[:], T.sh[:], T.h[:]).then_inc(S.qh, 1)
    v.wait_ge(S.ld_w2, 16)
    v.quantize_mx(T.qw2[:], T.sw2[:], T.w2b[:]).then_inc(S.qw2, 1)
    v.wait_ge(S.yd, 1)
    v.tensor_copy(T.ysb[:], yp).then_inc(S.yc, 1)
